import numpy as np
import ml_dtypes


def mxq(x, axis, fmt="e4m3"):
    dtype, down = {"e4m3": (ml_dtypes.float8_e4m3fn, 7), "e5m2": (ml_dtypes.float8_e5m2, 14)}[fmt]
    v = np.moveaxis(np.asarray(x, np.float32).astype(ml_dtypes.bfloat16).astype(np.float64), axis, -1)
    blocks = v.reshape(v.shape[:-1] + (-1, 32))
    amax = np.abs(blocks).max(-1, keepdims=True)
    byte = np.maximum(np.where(amax > 0, np.frexp(amax)[1] - 1 + 127, 0) - down, 1)
    scale = np.exp2(byte - 127.0)
    codes = (blocks / scale).astype(np.float32).astype(dtype).astype(np.float64)
    return np.moveaxis((codes * scale).reshape(v.shape), -1, axis)


WIDE = False


def mx_kscale(k):
    if not WIDE:
        return np.ones(k)
    levels = np.array([10, -10, 5, -5, 0])
    if k % 512:
        return np.exp2(np.random.permutation(np.resize(levels, k // 32))).repeat(32)
    a = np.empty((k // 512, 16))
    for p in range(k // 512):
        a[p, :8] = np.random.permutation(np.resize(levels, 8))
        for g in range(8):
            far = levels[np.abs(levels - a[p, g]) >= 10]
            a[p, g + 8] = far[np.random.randint(len(far))]
    return np.exp2(a.ravel()).repeat(32)


def f64(x):
    return np.asarray(x).astype(np.float64)


def striped(idx):
    return np.tile(idx.reshape(-1, 16).T, (8, 1)).astype(np.uint16)


def unstriped(offs):
    return offs[:16].T.reshape(-1).astype(np.int64)


def pack_weight(w):
    k, n = w.shape
    w = f64(np.asarray(w, np.float32).astype(ml_dtypes.bfloat16)).reshape(k // 32, 32, n)
    amax = np.abs(w).max(1)
    byte = np.clip(np.where(amax > 0, np.frexp(amax)[1] - 1 + 127 - 7, 1), 1, 254)
    scaled = (w * np.exp2(127.0 - byte)[:, None, :]).reshape(k, n).astype(np.float32)
    words = np.ascontiguousarray(scaled.reshape(k // 512, 128, 4, n).transpose(0, 1, 3, 2)).astype(ml_dtypes.float8_e4m3fn).view(np.uint8)
    return words, np.ascontiguousarray(byte.astype(np.uint8).reshape(k // 512, 16, n))


def unpack_weight(words, scales):
    g, p, n, _ = words.shape
    vals = np.ascontiguousarray(words).view(ml_dtypes.float8_e4m3fn).astype(np.float64) * np.repeat(np.exp2(scales.astype(np.float64) - 127.0), 8, axis=1)[..., None]
    return vals.transpose(0, 1, 3, 2).reshape(g * 512, n)


def relu(v):
    return np.maximum(v, 0.0)


K, T, D, N = 512, 1024, 4, 128
P = 2 ** 7


def setup_inputs():
    n = np.random.standard_normal
    s = mx_kscale(K)[:, None]
    packed_xT = pack_weight(n((K, T)) * s)
    return {
        "x_words": packed_xT[0],
        "x_scales": packed_xT[1],
        "w1": (n((K, N)) / np.sqrt(K) / s).astype(np.float32),
        "gate": (np.tile(np.random.uniform(0.2, 1.0, (D, 1, T)) / np.sqrt(D), (1, P, 1))).astype(np.float32),
        "pos1": striped(np.random.permutation(T)),
        "pos2": striped(np.random.permutation(T)),
        "pos3": striped(np.random.permutation(T)),
        "pos4": striped(np.random.permutation(T)),
    }


def reference(x_words, x_scales, w1, gate, pos1, pos2, pos3, pos4):
    xq = unpack_weight(x_words, x_scales)
    y = relu(mxq(f64(w1), 0, "e4m3").T @ xq)
    return y + (y[:, unstriped(pos1)] - y) * f64(gate)[0, :1] + (y[:, unstriped(pos2)] - y) * f64(gate)[1, :1] + (y[:, unstriped(pos3)] - y) * f64(gate)[2, :1] + (y[:, unstriped(pos4)] - y) * f64(gate)[3, :1]

@@ -1,0 +1,195 @@
+from contextlib import ExitStack
+
+import concourse.mybir as mybir
+from concourse.masks import make_identity
+
+K, T, D, N = 512, 1024, 4, 128
+FLOPS = 2 * K * T * N
+
+F32 = mybir.dt.float32
+BF16 = mybir.dt.bfloat16
+I32 = mybir.dt.int32
+U32 = mybir.dt.uint32
+U16 = mybir.dt.uint16
+U8 = mybir.dt.uint8
+FP8X4 = mybir.dt.float8_e4m3fn_x4
+MULT = mybir.AluOpType.mult
+ADD = mybir.AluOpType.add
+COPY = mybir.ActivationFunctionType.Copy
+RELU = mybir.ActivationFunctionType.Relu
+
+P = 128
+PACK = 4
+QUARTER = 256
+HALF = 512
+BLOCKS = T // P
+
+
+def tile_picked_wgrand_relu_l_kernel(
+    tc, x_words, x_scales, w1, gate, pos1, pos2, pos3, pos4, out
+):
+    nc = tc.nc
+    with ExitStack() as ctx:
+        sb = ctx.enter_context(tc.tile_pool(name="sb", bufs=1))
+        ps = ctx.enter_context(tc.psum_pool(name="ps", bufs=1))
+        banks = [ps.tile([P, HALF], F32, name="bank%d" % b) for b in range(8)]
+        col_banks = banks[0:4]
+        yt_banks = banks[4:6]
+        sum_banks = banks[6:8]
+
+        x_sc = sb.tile([P, T], U8, align_bytes=64)
+        g_rows = sb.tile([P, D, P], F32)
+        nc.gpsimd.memset(g_rows[:], 0.0)
+
+        w_raw = sb.tile([P, PACK, N], F32)
+        nc.sync.dma_start(out=w_raw[:], in_=w1.rearrange("(p j) m -> p j m", j=PACK))
+        x_flat = x_words[0].rearrange("p c r -> p (c r)").bitcast(I32)
+        x_w = []
+        for h in range(2):
+            words = sb.tile([P, HALF], I32, name="x_w%d" % h, align_bytes=64)
+            nc.sync.dma_start(out=words[:], in_=x_flat[:, h * HALF : (h + 1) * HALF])
+            x_w.append(words)
+        for q in range(4):
+            nc.scalar.dma_start(
+                out=x_sc[32 * q : 32 * q + 4, :].bitcast(I32),
+                in_=x_scales[0, 4 * q : 4 * q + 4, :].bitcast(I32),
+            )
+        nc.scalar.dma_start(
+            out=g_rows[0:BLOCKS, :, :], in_=gate[:, 0, :].rearrange("d (b i) -> b d i", i=P)
+        )
+
+        ident = sb.tile([P, P], F32)
+        make_identity(nc, ident[:])
+        warm = sb.tile([P, 8], F32)
+        nc.vector.memset(warm[:, 0:4], 0.0)
+        nc.scalar.activation(warm[:, 4:8], warm[:, 0:4], RELU)
+
+        lists = []
+        gates = []
+        for d, pos in enumerate((pos1, pos2, pos3, pos4)):
+            lst = sb.tile([P, T // 16], U16, name="list%d" % d)
+            nc.sync.dma_start(lst[:], pos)
+            lists.append(lst)
+            g = sb.tile([P, T], F32, name="gate%d" % d)
+            nc.sync.dma_start(out=g[:], in_=gate[d])
+            gates.append(g)
+
+        w_bf = sb.tile([P, N, PACK], BF16, align_bytes=64)
+        nc.vector.tensor_copy(
+            out=w_bf[:].rearrange("p (c i) t -> p c t i", i=4),
+            in_=w_raw[:].rearrange("p t (c i) -> p c t i", i=4),
+        )
+        w_q = sb.tile([P, N], U32, align_bytes=64)
+        w_sc = sb.tile([P, N], U8, align_bytes=64)
+        nc.vector.quantize_mx(
+            out=w_q[:].bitcast(FP8X4), scales=w_sc[:], in_=w_bf[:].rearrange("p m t -> p (m t)")
+        )
+
+        def turn(dst, src, start, stop):
+            nc.tensor.matmul(dst, src, ident[:], start=start, stop=stop, is_transpose=True)
+
+        y = sb.tile([P, T], F32)
+        for q in range(4):
+            cols = slice(q * QUARTER, (q + 1) * QUARTER)
+            acc = col_banks[q][:, 0:QUARTER]
+            nc.tensor.matmul_mx(
+                out=acc,
+                lhsT=w_q[:].bitcast(FP8X4),
+                lhsT_scale=w_sc[:],
+                rhs=x_w[q // 2][:, (q % 2) * QUARTER : (q % 2 + 1) * QUARTER].bitcast(FP8X4),
+                rhs_scale=x_sc[:, cols],
+                start=True,
+                stop=True,
+            )
+            if q % 2 == 0:
+                nc.scalar.activation(y[:, cols], acc, RELU)
+            else:
+                nc.vector.tensor_scalar_max(y[:, cols], acc, 0.0)
+
+        for d in range(D):
+            turn(sum_banks[0][:, 0:P], g_rows[:, d, :], d == 0, d == D - 1)
+        keep = sb.tile([P, BLOCKS], F32)
+        nc.scalar.activation(keep[:], sum_banks[0][:, 0:BLOCKS], COPY, bias=1.0, scale=-1.0)
+
+        own_t = [sb.tile([P, HALF], F32, name="own_t%d" % h) for h in range(2)]
+        for h in (1, 0):
+            for i in range(4):
+                b = 4 * h + i
+                turn(yt_banks[h][:, i * P : (i + 1) * P], y[:, b * P : (b + 1) * P], True, True)
+            for i in range(4):
+                b = 4 * h + i
+                nc.scalar.activation(
+                    own_t[h][:, i * P : (i + 1) * P],
+                    yt_banks[h][:, i * P : (i + 1) * P],
+                    COPY,
+                    scale=keep[:, b : b + 1],
+                )
+
+        def gather(d, c0, width):
+            prod = sb.tile([P, width], F32, name="prod%d_%d" % (d, c0))
+            nc.vector.tensor_tensor(
+                prod[:],
+                y[:].indirect(lists[d][:, c0 // 16 : (c0 + width) // 16]),
+                gates[d][:, c0 : c0 + width],
+                MULT,
+            )
+            return prod
+
+        def turn_in(bank, prod, off, blocks, first, last):
+            for i in range(blocks):
+                turn(
+                    bank[:, i * P : (i + 1) * P],
+                    prod[:, off + i * P : off + (i + 1) * P],
+                    first and i == 0,
+                    last and i == blocks - 1,
+                )
+
+        def own_back(q):
+            for i in range(2):
+                c = (q % 2) * QUARTER + i * P
+                turn(col_banks[q][:, i * P : (i + 1) * P], own_t[q // 2][:, c : c + P], i == 0, False)
+
+        def sum_back(q, sum_t, off):
+            for i in range(2):
+                c = off + i * P
+                turn(col_banks[q][:, i * P : (i + 1) * P], sum_t[:, c : c + P], False, i == 1)
+
+        for d in range(D - 1):
+            prod = gather(d, HALF, HALF)
+            turn_in(sum_banks[0], prod, 0, 4, d == 0, d == D - 2)
+            if d == 0:
+                own_back(2)
+                own_back(3)
+            if d == 1:
+                own_back(0)
+                own_back(1)
+        sum_up = sb.tile([P, HALF], F32)
+        nc.scalar.copy(sum_up[:], sum_banks[0][:])
+
+        low_banks = (sum_banks[1], yt_banks[1])
+        for d in range(D - 1):
+            prod = gather(d, 0, HALF)
+            for q in range(2):
+                turn_in(low_banks[q], prod, q * QUARTER, 2, d == 0, False)
+            if d == 0:
+                sum_back(2, sum_up, 0)
+                sum_back(3, sum_up, QUARTER)
+
+        sums = []
+        for q in range(2):
+            prod = gather(D - 1, q * QUARTER, QUARTER)
+            turn_in(low_banks[q], prod, 0, 2, False, True)
+            sum_low = sb.tile([P, QUARTER], F32, name="sum_low%d" % q)
+            nc.scalar.copy(sum_low[:], low_banks[q][:, 0:QUARTER])
+            sums.append(sum_low)
+        for q in range(2):
+            sum_back(q, sums[q], 0)
+            res = sb.tile([P, QUARTER], F32, name="res%d" % q)
+            nc.scalar.copy(res[:], col_banks[q][:, 0:QUARTER])
+            nc.sync.dma_start(out=out[:, q * QUARTER : (q + 1) * QUARTER], in_=res[:])
+
+        prods = [gather(D - 1, q * QUARTER, QUARTER) for q in (2, 3)]
+        for q in (2, 3):
+            res = sb.tile([P, QUARTER], F32, name="res%d" % q)
+            nc.vector.tensor_tensor(res[:], col_banks[q][:, 0:QUARTER], prods[q - 2][:], ADD)
+            nc.sync.dma_start(out=out[:, q * QUARTER : (q + 1) * QUARTER], in_=res[:])

@@ -23,6 +23,7 @@ PACK = 4
 QUARTER = 256
 HALF = 512
 BLOCKS = T // P
+LOW = 512
 
 
 def tile_picked_wgrand_relu_l_kernel(
@@ -43,36 +44,35 @@ def tile_picked_wgrand_relu_l_kernel(
 
         w_raw = sb.tile([P, PACK, N], F32)
         nc.sync.dma_start(out=w_raw[:], in_=w1.rearrange("(p j) m -> p j m", j=PACK))
+        for q in range(4):
+            (nc.sync if q < 2 else nc.scalar).dma_start(
+                out=x_sc[32 * q : 32 * q + 4, :].bitcast(I32),
+                in_=x_scales[0, 4 * q : 4 * q + 4, :].bitcast(I32),
+            )
         x_flat = x_words[0].rearrange("p c r -> p (c r)").bitcast(I32)
         x_w = []
         for h in range(2):
             words = sb.tile([P, HALF], I32, name="x_w%d" % h, align_bytes=64)
             nc.sync.dma_start(out=words[:], in_=x_flat[:, h * HALF : (h + 1) * HALF])
             x_w.append(words)
-        for q in range(4):
-            nc.scalar.dma_start(
-                out=x_sc[32 * q : 32 * q + 4, :].bitcast(I32),
-                in_=x_scales[0, 4 * q : 4 * q + 4, :].bitcast(I32),
-            )
-        nc.scalar.dma_start(
-            out=g_rows[0:BLOCKS, :, :], in_=gate[:, 0, :].rearrange("d (b i) -> b d i", i=P)
-        )
 
         ident = sb.tile([P, P], F32)
         make_identity(nc, ident[:])
-        warm = sb.tile([P, 8], F32)
-        nc.vector.memset(warm[:, 0:4], 0.0)
-        nc.scalar.activation(warm[:, 4:8], warm[:, 0:4], RELU)
 
         lists = []
-        gates = []
+        gates = [[], []]
         for d, pos in enumerate((pos1, pos2, pos3, pos4)):
             lst = sb.tile([P, T // 16], U16, name="list%d" % d)
             nc.sync.dma_start(lst[:], pos)
             lists.append(lst)
-            g = sb.tile([P, T], F32, name="gate%d" % d)
-            nc.sync.dma_start(out=g[:], in_=gate[d])
-            gates.append(g)
+            for h in range(2):
+                g = sb.tile([P, HALF], F32, name="gate%d_%d" % (d, h))
+                nc.sync.dma_start(out=g[:], in_=gate[d, :, h * HALF : (h + 1) * HALF])
+                gates[h].append(g)
+                if d == 0 and h == 0:
+                    nc.sync.dma_start(
+                        out=g_rows[0:BLOCKS, :, :], in_=gate[:, 0, :].rearrange("d (b i) -> b d i", i=P)
+                    )
 
         w_bf = sb.tile([P, N, PACK], BF16, align_bytes=64)
         nc.vector.tensor_copy(
@@ -89,22 +89,24 @@ def tile_picked_wgrand_relu_l_kernel(
             nc.tensor.matmul(dst, src, ident[:], start=start, stop=stop, is_transpose=True)
 
         y = sb.tile([P, T], F32)
-        for q in range(4):
-            cols = slice(q * QUARTER, (q + 1) * QUARTER)
-            acc = col_banks[q][:, 0:QUARTER]
+        c0 = 0
+        for q, width in enumerate((256, 256, 256, 128, 128)):
+            cols = slice(c0, c0 + width)
+            acc = (col_banks + [sum_banks[1]])[q][:, 0:width]
             nc.tensor.matmul_mx(
                 out=acc,
                 lhsT=w_q[:].bitcast(FP8X4),
                 lhsT_scale=w_sc[:],
-                rhs=x_w[q // 2][:, (q % 2) * QUARTER : (q % 2 + 1) * QUARTER].bitcast(FP8X4),
+                rhs=x_w[c0 // HALF][:, c0 % HALF : c0 % HALF + width].bitcast(FP8X4),
                 rhs_scale=x_sc[:, cols],
                 start=True,
                 stop=True,
             )
-            if q % 2 == 0:
-                nc.scalar.activation(y[:, cols], acc, RELU)
-            else:
+            if q in (0, 2):
                 nc.vector.tensor_scalar_max(y[:, cols], acc, 0.0)
+            else:
+                nc.scalar.activation(y[:, cols], acc, RELU)
+            c0 = c0 + width
 
         for d in range(D):
             turn(sum_banks[0][:, 0:P], g_rows[:, d, :], d == 0, d == D - 1)
@@ -112,7 +114,7 @@ def tile_picked_wgrand_relu_l_kernel(
         nc.scalar.activation(keep[:], sum_banks[0][:, 0:BLOCKS], COPY, bias=1.0, scale=-1.0)
 
         own_t = [sb.tile([P, HALF], F32, name="own_t%d" % h) for h in range(2)]
-        for h in (1, 0):
+        for h in range(2):
             for i in range(4):
                 b = 4 * h + i
                 turn(yt_banks[h][:, i * P : (i + 1) * P], y[:, b * P : (b + 1) * P], True, True)
@@ -130,7 +132,7 @@ def tile_picked_wgrand_relu_l_kernel(
             nc.vector.tensor_tensor(
                 prod[:],
                 y[:].indirect(lists[d][:, c0 // 16 : (c0 + width) // 16]),
-                gates[d][:, c0 : c0 + width],
+                gates[0][d][:, c0 : c0 + width] if c0 < LOW else gates[1][d][:, c0 - LOW : c0 - LOW + width],
                 MULT,
             )
             return prod
@@ -144,52 +146,38 @@ def tile_picked_wgrand_relu_l_kernel(
                     last and i == blocks - 1,
                 )
 
-        def own_back(q):
-            for i in range(2):
-                c = (q % 2) * QUARTER + i * P
-                turn(col_banks[q][:, i * P : (i + 1) * P], own_t[q // 2][:, c : c + P], i == 0, False)
+        out_banks = (col_banks[0], col_banks[2])
 
-        def sum_back(q, sum_t, off):
-            for i in range(2):
-                c = off + i * P
-                turn(col_banks[q][:, i * P : (i + 1) * P], sum_t[:, c : c + P], False, i == 1)
+        def own_back(h):
+            for i in range(4):
+                blk = slice(i * P, (i + 1) * P)
+                turn(out_banks[h][:, blk], own_t[h][:, blk], i == 0, False)
+
+        def sum_back(h):
+            sum_t = sb.tile([P, HALF], F32, name="sum_t%d" % h)
+            nc.scalar.copy(sum_t[:], sum_banks[h][:])
+            for i in range(4):
+                blk = slice(i * P, (i + 1) * P)
+                turn(out_banks[h][:, blk], sum_t[:, blk], False, i == 3)
 
         for d in range(D - 1):
-            prod = gather(d, HALF, HALF)
-            turn_in(sum_banks[0], prod, 0, 4, d == 0, d == D - 2)
-            if d == 0:
-                own_back(2)
-                own_back(3)
-            if d == 1:
-                own_back(0)
-                own_back(1)
-        sum_up = sb.tile([P, HALF], F32)
-        nc.scalar.copy(sum_up[:], sum_banks[0][:])
+            for h in range(2):
+                prod = gather(d, h * HALF, HALF)
+                turn_in(sum_banks[h], prod, 0, 4, d == 0, d == D - 2)
+                if d == 1:
+                    own_back(h)
+        for h in range(2):
+            sum_back(h)
 
-        low_banks = (sum_banks[1], yt_banks[1])
-        for d in range(D - 1):
-            prod = gather(d, 0, HALF)
-            for q in range(2):
-                turn_in(low_banks[q], prod, q * QUARTER, 2, d == 0, False)
-            if d == 0:
-                sum_back(2, sum_up, 0)
-                sum_back(3, sum_up, QUARTER)
+        def finish(c0, width, prod):
+            res = sb.tile([P, width], F32, name="res%d" % c0)
+            nc.vector.tensor_tensor(res[:], out_banks[c0 // HALF][:, c0 % HALF : c0 % HALF + width], prod[:], ADD)
+            nc.sync.dma_start(out=out[:, c0 : c0 + width], in_=res[:])
 
-        sums = []
-        for q in range(2):
-            prod = gather(D - 1, q * QUARTER, QUARTER)
-            turn_in(low_banks[q], prod, 0, 2, False, True)
-            sum_low = sb.tile([P, QUARTER], F32, name="sum_low%d" % q)
-            nc.scalar.copy(sum_low[:], low_banks[q][:, 0:QUARTER])
-            sums.append(sum_low)
-        for q in range(2):
-            sum_back(q, sums[q], 0)
-            res = sb.tile([P, QUARTER], F32, name="res%d" % q)
-            nc.scalar.copy(res[:], col_banks[q][:, 0:QUARTER])
-            nc.sync.dma_start(out=out[:, q * QUARTER : (q + 1) * QUARTER], in_=res[:])
-
-        prods = [gather(D - 1, q * QUARTER, QUARTER) for q in (2, 3)]
-        for q in (2, 3):
-            res = sb.tile([P, QUARTER], F32, name="res%d" % q)
-            nc.vector.tensor_tensor(res[:], col_banks[q][:, 0:QUARTER], prods[q - 2][:], ADD)
-            nc.sync.dma_start(out=out[:, q * QUARTER : (q + 1) * QUARTER], in_=res[:])
+        ends = ((0, HALF), (HALF, QUARTER), (HALF + QUARTER, QUARTER))
+        prods = []
+        for i, (c0, width) in enumerate(ends):
+            prods.append(gather(D - 1, c0, width))
+            if i > 0:
+                finish(*ends[i - 1], prods[i - 1])
+        finish(*ends[-1], prods[-1])

@@ -146,38 +146,37 @@ def tile_picked_wgrand_relu_l_kernel(
                     last and i == blocks - 1,
                 )
 
-        out_banks = (col_banks[0], col_banks[2])
+        part_banks = sum_banks + yt_banks
 
-        def own_back(h):
-            for i in range(4):
-                blk = slice(i * P, (i + 1) * P)
-                turn(out_banks[h][:, blk], own_t[h][:, blk], i == 0, False)
+        def own_back(q):
+            for i in range(2):
+                c = (q % 2) * QUARTER + i * P
+                turn(col_banks[q][:, i * P : (i + 1) * P], own_t[q // 2][:, c : c + P], i == 0, False)
 
-        def sum_back(h):
-            sum_t = sb.tile([P, HALF], F32, name="sum_t%d" % h)
-            nc.scalar.copy(sum_t[:], sum_banks[h][:])
-            for i in range(4):
-                blk = slice(i * P, (i + 1) * P)
-                turn(out_banks[h][:, blk], sum_t[:, blk], False, i == 3)
-
-        for d in range(D - 1):
+        for d in range(2):
             for h in range(2):
                 prod = gather(d, h * HALF, HALF)
-                turn_in(sum_banks[h], prod, 0, 4, d == 0, d == D - 2)
-                if d == 1:
-                    own_back(h)
-        for h in range(2):
-            sum_back(h)
+                for q in range(2):
+                    turn_in(part_banks[2 * h + q], prod, q * QUARTER, 2, d == 0, False)
+                if d != h:
+                    own_back(2 * d)
+                    own_back(2 * d + 1)
 
-        def finish(c0, width, prod):
-            res = sb.tile([P, width], F32, name="res%d" % c0)
-            nc.vector.tensor_tensor(res[:], out_banks[c0 // HALF][:, c0 % HALF : c0 % HALF + width], prod[:], ADD)
-            nc.sync.dma_start(out=out[:, c0 : c0 + width], in_=res[:])
+        parts = []
+        for q in range(4):
+            prod = gather(2, q * QUARTER, QUARTER)
+            turn_in(part_banks[q], prod, 0, 2, False, True)
+            part = sb.tile([P, QUARTER], F32, name="part%d" % q)
+            nc.scalar.copy(part[:], part_banks[q][:, 0:QUARTER])
+            parts.append(part)
+        for q in range(4):
+            for i in range(2):
+                blk = slice(i * P, (i + 1) * P)
+                turn(col_banks[q][:, blk], parts[q][:, blk], False, i == 1)
 
-        ends = ((0, HALF), (HALF, QUARTER), (HALF + QUARTER, QUARTER))
-        prods = []
-        for i, (c0, width) in enumerate(ends):
-            prods.append(gather(D - 1, c0, width))
-            if i > 0:
-                finish(*ends[i - 1], prods[i - 1])
-        finish(*ends[-1], prods[-1])
+        prods = [gather(D - 1, h * HALF, HALF) for h in range(2)]
+        for q in range(4):
+            res = sb.tile([P, QUARTER], F32, name="res%d" % q)
+            c = (q % 2) * QUARTER
+            nc.vector.tensor_tensor(res[:], col_banks[q][:, 0:QUARTER], prods[q // 2][:, c : c + QUARTER], ADD)
+            nc.sync.dma_start(out=out[:, q * QUARTER : (q + 1) * QUARTER], in_=res[:])

@@ -20,10 +20,15 @@ RELU = mybir.ActivationFunctionType.Relu
 
 P = 128
 PACK = 4
-QUARTER = 256
-HALF = 512
+BANK = 512
 BLOCKS = T // P
-LOW = 512
+BLOCKS_A_BANK = BANK // P
+LIST_ROWS = 16
+
+PASSES = ((256, True), (256, False), (256, True), (128, False), (128, False))
+
+PIECES = ((0, 3), (3, 2), (5, 2), (7, 1))
+EARLY = PIECES[0][1] * P
 
 
 def tile_picked_wgrand_relu_l_kernel(
@@ -33,17 +38,19 @@ def tile_picked_wgrand_relu_l_kernel(
     with ExitStack() as ctx:
         sb = ctx.enter_context(tc.tile_pool(name="sb", bufs=1))
         ps = ctx.enter_context(tc.psum_pool(name="ps", bufs=1))
-        banks = [ps.tile([P, HALF], F32, name="bank%d" % b) for b in range(8)]
-        col_banks = banks[0:4]
-        yt_banks = banks[4:6]
-        sum_banks = banks[6:8]
+        banks = [ps.tile([P, BANK], F32, name="bank%d" % b) for b in range(8)]
+        mx_banks = banks[0:4] + [banks[7]]
+        y_t_banks = banks[4:6]
+        gate_bank = banks[6]
+        out_banks = banks[0:4]
+        sum_banks = [banks[6], banks[7], banks[4], banks[5]]
 
         x_sc = sb.tile([P, T], U8, align_bytes=64)
-        g_rows = sb.tile([P, D, P], F32)
-        nc.gpsimd.memset(g_rows[:], 0.0)
+        gate_rows = sb.tile([P, D, P], F32)
+        nc.gpsimd.memset(gate_rows[:], 0.0)
 
         w_raw = sb.tile([P, PACK, N], F32)
-        nc.sync.dma_start(out=w_raw[:], in_=w1.rearrange("(p j) m -> p j m", j=PACK))
+        nc.sync.dma_start(out=w_raw[:], in_=w1.rearrange("(p t) m -> p t m", t=PACK))
         for q in range(4):
             (nc.sync if q < 2 else nc.scalar).dma_start(
                 out=x_sc[32 * q : 32 * q + 4, :].bitcast(I32),
@@ -52,27 +59,29 @@ def tile_picked_wgrand_relu_l_kernel(
         x_flat = x_words[0].rearrange("p c r -> p (c r)").bitcast(I32)
         x_w = []
         for h in range(2):
-            words = sb.tile([P, HALF], I32, name="x_w%d" % h, align_bytes=64)
-            nc.sync.dma_start(out=words[:], in_=x_flat[:, h * HALF : (h + 1) * HALF])
+            words = sb.tile([P, T // 2], I32, name="x_w%d" % h, align_bytes=64)
+            nc.sync.dma_start(out=words[:], in_=x_flat[:, h * T // 2 : (h + 1) * T // 2])
             x_w.append(words)
 
         ident = sb.tile([P, P], F32)
         make_identity(nc, ident[:])
 
-        lists = []
-        gates = [[], []]
+        lists, gates_early, gates_late = [], [], []
         for d, pos in enumerate((pos1, pos2, pos3, pos4)):
-            lst = sb.tile([P, T // 16], U16, name="list%d" % d)
-            nc.sync.dma_start(lst[:], pos)
-            lists.append(lst)
-            for h in range(2):
-                g = sb.tile([P, HALF], F32, name="gate%d_%d" % (d, h))
-                nc.sync.dma_start(out=g[:], in_=gate[d, :, h * HALF : (h + 1) * HALF])
-                gates[h].append(g)
-                if d == 0 and h == 0:
-                    nc.sync.dma_start(
-                        out=g_rows[0:BLOCKS, :, :], in_=gate[:, 0, :].rearrange("d (b i) -> b d i", i=P)
-                    )
+            offsets = sb.tile([P, T // LIST_ROWS], U16, name="list%d" % d)
+            nc.sync.dma_start(offsets[:], pos)
+            lists.append(offsets)
+            early = sb.tile([P, EARLY], F32, name="gate_early%d" % d)
+            nc.sync.dma_start(out=early[:], in_=gate[d, :, 0:EARLY])
+            gates_early.append(early)
+            if d == 0:
+                nc.sync.dma_start(
+                    out=gate_rows[0:BLOCKS, :, :], in_=gate[:, 0, :].rearrange("d (b i) -> b d i", i=P)
+                )
+        for d in range(D):
+            late = sb.tile([P, T - EARLY], F32, name="gate_late%d" % d)
+            nc.sync.dma_start(out=late[:], in_=gate[d, :, EARLY:T])
+            gates_late.append(late)
 
         w_bf = sb.tile([P, N, PACK], BF16, align_bytes=64)
         nc.vector.tensor_copy(
@@ -85,98 +94,114 @@ def tile_picked_wgrand_relu_l_kernel(
             out=w_q[:].bitcast(FP8X4), scales=w_sc[:], in_=w_bf[:].rearrange("p m t -> p (m t)")
         )
 
-        def turn(dst, src, start, stop):
-            nc.tensor.matmul(dst, src, ident[:], start=start, stop=stop, is_transpose=True)
-
         y = sb.tile([P, T], F32)
-        c0 = 0
-        for q, width in enumerate((256, 256, 256, 128, 128)):
-            cols = slice(c0, c0 + width)
-            acc = (col_banks + [sum_banks[1]])[q][:, 0:width]
+        first = 0
+        for bank, (width, on_vector) in zip(mx_banks, PASSES):
+            nodes = slice(first, first + width)
+            half, within = divmod(first, T // 2)
             nc.tensor.matmul_mx(
-                out=acc,
+                out=bank[:, 0:width],
                 lhsT=w_q[:].bitcast(FP8X4),
                 lhsT_scale=w_sc[:],
-                rhs=x_w[c0 // HALF][:, c0 % HALF : c0 % HALF + width].bitcast(FP8X4),
-                rhs_scale=x_sc[:, cols],
+                rhs=x_w[half][:, within : within + width].bitcast(FP8X4),
+                rhs_scale=x_sc[:, nodes],
                 start=True,
                 stop=True,
             )
-            if q in (0, 2):
-                nc.vector.tensor_scalar_max(y[:, cols], acc, 0.0)
+            if on_vector:
+                nc.vector.tensor_scalar_max(y[:, nodes], bank[:, 0:width], 0.0)
             else:
-                nc.scalar.activation(y[:, cols], acc, RELU)
-            c0 = c0 + width
+                nc.scalar.activation(y[:, nodes], bank[:, 0:width], RELU)
+            first = first + width
+
+        def block(i):
+            return slice(i * P, (i + 1) * P)
+
+        def turn(dst, src, start, stop):
+            nc.tensor.matmul(dst, src, ident[:], start=start, stop=stop, is_transpose=True)
 
         for d in range(D):
-            turn(sum_banks[0][:, 0:P], g_rows[:, d, :], d == 0, d == D - 1)
+            turn(gate_bank[:, block(0)], gate_rows[:, d, :], d == 0, d == D - 1)
         keep = sb.tile([P, BLOCKS], F32)
-        nc.scalar.activation(keep[:], sum_banks[0][:, 0:BLOCKS], COPY, bias=1.0, scale=-1.0)
+        nc.scalar.activation(keep[:], gate_bank[:, 0:BLOCKS], COPY, bias=1.0, scale=-1.0)
 
-        own_t = [sb.tile([P, HALF], F32, name="own_t%d" % h) for h in range(2)]
-        for h in range(2):
-            for i in range(4):
-                b = 4 * h + i
-                turn(yt_banks[h][:, i * P : (i + 1) * P], y[:, b * P : (b + 1) * P], True, True)
-            for i in range(4):
-                b = 4 * h + i
-                nc.scalar.activation(
-                    own_t[h][:, i * P : (i + 1) * P],
-                    yt_banks[h][:, i * P : (i + 1) * P],
-                    COPY,
-                    scale=keep[:, b : b + 1],
-                )
+        own_t = []
+        for h, bank in enumerate(y_t_banks):
+            scaled = sb.tile([P, BANK], F32, name="own_t%d" % h)
+            for i in range(BLOCKS_A_BANK):
+                turn(bank[:, block(i)], y[:, block(BLOCKS_A_BANK * h + i)], True, True)
+            for i in range(BLOCKS_A_BANK):
+                b = BLOCKS_A_BANK * h + i
+                nc.scalar.activation(scaled[:, block(i)], bank[:, block(i)], COPY, scale=keep[:, b : b + 1])
+            own_t.append(scaled)
 
-        def gather(d, c0, width):
-            prod = sb.tile([P, width], F32, name="prod%d_%d" % (d, c0))
-            nc.vector.tensor_tensor(
-                prod[:],
-                y[:].indirect(lists[d][:, c0 // 16 : (c0 + width) // 16]),
-                gates[0][d][:, c0 : c0 + width] if c0 < LOW else gates[1][d][:, c0 - LOW : c0 - LOW + width],
-                MULT,
-            )
+        def product(d, start, width):
+            prod = sb.tile([P, width], F32, name="prod%d_%d" % (d, start))
+            if start < EARLY:
+                gates = gates_early[d][:]
+            else:
+                gates = gates_late[d][:, start - EARLY : start - EARLY + width]
+            entries = lists[d][:, start // LIST_ROWS : (start + width) // LIST_ROWS]
+            nc.vector.tensor_tensor(prod[:], y[:].indirect(entries), gates, MULT)
             return prod
 
-        def turn_in(bank, prod, off, blocks, first, last):
+        def add_turned(q, prod, skip, opens, closes):
+            blocks = PIECES[q][1]
             for i in range(blocks):
                 turn(
-                    bank[:, i * P : (i + 1) * P],
-                    prod[:, off + i * P : off + (i + 1) * P],
-                    first and i == 0,
-                    last and i == blocks - 1,
+                    sum_banks[q][:, block(i)],
+                    prod[:, block(skip + i)],
+                    opens and i == 0,
+                    closes and i == blocks - 1,
                 )
 
-        part_banks = sum_banks + yt_banks
-
         def own_back(q):
-            for i in range(2):
-                c = (q % 2) * QUARTER + i * P
-                turn(col_banks[q][:, i * P : (i + 1) * P], own_t[q // 2][:, c : c + P], i == 0, False)
+            b0, blocks = PIECES[q]
+            for i in range(blocks):
+                h, j = divmod(b0 + i, BLOCKS_A_BANK)
+                turn(out_banks[q][:, block(i)], own_t[h][:, block(j)], i == 0, False)
+
+        def sums_out(q):
+            sums = sb.tile([P, PIECES[q][1] * P], F32, name="sums%d" % q)
+            nc.scalar.copy(sums[:], sum_banks[q][:, 0 : PIECES[q][1] * P])
+            return sums
+
+        def sums_back(q, sums):
+            blocks = PIECES[q][1]
+            for i in range(blocks):
+                turn(out_banks[q][:, block(i)], sums[:, block(i)], False, i == blocks - 1)
+
+        late_pieces = range(1, len(PIECES))
+
+        for d in range(D):
+            add_turned(0, product(d, 0, EARLY), 0, d == 0, d == D - 1)
+            if d in (1, 2):
+                own_back(2 * d - 2)
+                own_back(2 * d - 1)
 
         for d in range(2):
-            for h in range(2):
-                prod = gather(d, h * HALF, HALF)
-                for q in range(2):
-                    turn_in(part_banks[2 * h + q], prod, q * QUARTER, 2, d == 0, False)
-                if d != h:
-                    own_back(2 * d)
-                    own_back(2 * d + 1)
+            prod = product(d, EARLY, T - EARLY)
+            for q in late_pieces:
+                add_turned(q, prod, PIECES[q][0] - PIECES[0][1], d == 0, False)
+            if d == 0:
+                sums_back(0, sums_out(0))
+                result = sb.tile([P, EARLY], F32, name="result0")
+                nc.scalar.copy(result[:], out_banks[0][:, 0:EARLY])
+                nc.scalar.dma_start(out=out[:, 0:EARLY], in_=result[:])
 
-        parts = []
-        for q in range(4):
-            prod = gather(2, q * QUARTER, QUARTER)
-            turn_in(part_banks[q], prod, 0, 2, False, True)
-            part = sb.tile([P, QUARTER], F32, name="part%d" % q)
-            nc.scalar.copy(part[:], part_banks[q][:, 0:QUARTER])
-            parts.append(part)
-        for q in range(4):
-            for i in range(2):
-                blk = slice(i * P, (i + 1) * P)
-                turn(col_banks[q][:, blk], parts[q][:, blk], False, i == 1)
+        sums = {}
+        for q in late_pieces:
+            b0, blocks = PIECES[q]
+            add_turned(q, product(2, b0 * P, blocks * P), 0, False, True)
+            sums[q] = sums_out(q)
+        for q in late_pieces:
+            sums_back(q, sums[q])
 
-        prods = [gather(D - 1, h * HALF, HALF) for h in range(2)]
-        for q in range(4):
-            res = sb.tile([P, QUARTER], F32, name="res%d" % q)
-            c = (q % 2) * QUARTER
-            nc.vector.tensor_tensor(res[:], col_banks[q][:, 0:QUARTER], prods[q // 2][:, c : c + QUARTER], ADD)
-            nc.sync.dma_start(out=out[:, q * QUARTER : (q + 1) * QUARTER], in_=res[:])
+        prod = product(D - 1, EARLY, T - EARLY)
+        for q in late_pieces:
+            start, width = PIECES[q][0] * P, PIECES[q][1] * P
+            result = sb.tile([P, width], F32, name="result%d" % q)
+            nc.vector.tensor_tensor(
+                result[:], out_banks[q][:, 0:width], prod[:, start - EARLY : start - EARLY + width], ADD
+            )
+            nc.sync.dma_start(out=out[:, start : start + width], in_=result[:])

from contextlib import ExitStack

import concourse.mybir as mybir
from concourse.masks import make_identity

K, T, D, N = 512, 1024, 4, 128
FLOPS = 2 * K * T * N

F32 = mybir.dt.float32
BF16 = mybir.dt.bfloat16
I32 = mybir.dt.int32
U32 = mybir.dt.uint32
U16 = mybir.dt.uint16
U8 = mybir.dt.uint8
FP8X4 = mybir.dt.float8_e4m3fn_x4
MULT = mybir.AluOpType.mult
ADD = mybir.AluOpType.add
COPY = mybir.ActivationFunctionType.Copy
RELU = mybir.ActivationFunctionType.Relu

P = 128
PACK = 4
BANK = 512
BLOCKS = T // P
BLOCKS_A_BANK = BANK // P
LIST_ROWS = 16

PASSES = ((256, True), (256, False), (256, True), (128, False), (128, False))

PIECES = ((0, 3), (3, 2), (5, 2), (7, 1))
EARLY = PIECES[0][1] * P


def tile_picked_wgrand_relu_l_kernel(
    tc, x_words, x_scales, w1, gate, pos1, pos2, pos3, pos4, out
):
    nc = tc.nc
    with ExitStack() as ctx:
        sb = ctx.enter_context(tc.tile_pool(name="sb", bufs=1))
        ps = ctx.enter_context(tc.psum_pool(name="ps", bufs=1))
        banks = [ps.tile([P, BANK], F32, name="bank%d" % b) for b in range(8)]
        mx_banks = banks[0:4] + [banks[7]]
        y_t_banks = banks[4:6]
        gate_bank = banks[6]
        out_banks = banks[0:4]
        sum_banks = [banks[6], banks[7], banks[4], banks[5]]

        x_sc = sb.tile([P, T], U8, align_bytes=64)
        gate_rows = sb.tile([P, D, P], F32)
        nc.gpsimd.memset(gate_rows[:], 0.0)

        w_raw = sb.tile([P, PACK, N], F32)
        nc.sync.dma_start(out=w_raw[:], in_=w1.rearrange("(p t) m -> p t m", t=PACK))
        for q in range(4):
            (nc.sync if q < 2 else nc.scalar).dma_start(
                out=x_sc[32 * q : 32 * q + 4, :].bitcast(I32),
                in_=x_scales[0, 4 * q : 4 * q + 4, :].bitcast(I32),
            )
        x_flat = x_words[0].rearrange("p c r -> p (c r)").bitcast(I32)
        x_w = []
        for h in range(2):
            words = sb.tile([P, T // 2], I32, name="x_w%d" % h, align_bytes=64)
            nc.sync.dma_start(out=words[:], in_=x_flat[:, h * T // 2 : (h + 1) * T // 2])
            x_w.append(words)

        ident = sb.tile([P, P], F32)
        make_identity(nc, ident[:])

        lists, gates_early, gates_late = [], [], []
        for d, pos in enumerate((pos1, pos2, pos3, pos4)):
            offsets = sb.tile([P, T // LIST_ROWS], U16, name="list%d" % d)
            nc.sync.dma_start(offsets[:], pos)
            lists.append(offsets)
            early = sb.tile([P, EARLY], F32, name="gate_early%d" % d)
            nc.sync.dma_start(out=early[:], in_=gate[d, :, 0:EARLY])
            gates_early.append(early)
            if d == 0:
                nc.sync.dma_start(
                    out=gate_rows[0:BLOCKS, :, :], in_=gate[:, 0, :].rearrange("d (b i) -> b d i", i=P)
                )
        for d in range(D):
            late = sb.tile([P, T - EARLY], F32, name="gate_late%d" % d)
            nc.sync.dma_start(out=late[:], in_=gate[d, :, EARLY:T])
            gates_late.append(late)

        w_bf = sb.tile([P, N, PACK], BF16, align_bytes=64)
        nc.vector.tensor_copy(
            out=w_bf[:].rearrange("p (c i) t -> p c t i", i=4),
            in_=w_raw[:].rearrange("p t (c i) -> p c t i", i=4),
        )
        w_q = sb.tile([P, N], U32, align_bytes=64)
        w_sc = sb.tile([P, N], U8, align_bytes=64)
        nc.vector.quantize_mx(
            out=w_q[:].bitcast(FP8X4), scales=w_sc[:], in_=w_bf[:].rearrange("p m t -> p (m t)")
        )

        y = sb.tile([P, T], F32)
        first = 0
        for bank, (width, on_vector) in zip(mx_banks, PASSES):
            nodes = slice(first, first + width)
            half, within = divmod(first, T // 2)
            nc.tensor.matmul_mx(
                out=bank[:, 0:width],
                lhsT=w_q[:].bitcast(FP8X4),
                lhsT_scale=w_sc[:],
                rhs=x_w[half][:, within : within + width].bitcast(FP8X4),
                rhs_scale=x_sc[:, nodes],
                start=True,
                stop=True,
            )
            if on_vector:
                nc.vector.tensor_scalar_max(y[:, nodes], bank[:, 0:width], 0.0)
            else:
                nc.scalar.activation(y[:, nodes], bank[:, 0:width], RELU)
            first = first + width

        def block(i):
            return slice(i * P, (i + 1) * P)

        def turn(dst, src, start, stop):
            nc.tensor.matmul(dst, src, ident[:], start=start, stop=stop, is_transpose=True)

        for d in range(D):
            turn(gate_bank[:, block(0)], gate_rows[:, d, :], d == 0, d == D - 1)
        keep = sb.tile([P, BLOCKS], F32)
        nc.scalar.activation(keep[:], gate_bank[:, 0:BLOCKS], COPY, bias=1.0, scale=-1.0)

        own_t = []
        for h, bank in enumerate(y_t_banks):
            scaled = sb.tile([P, BANK], F32, name="own_t%d" % h)
            for i in range(BLOCKS_A_BANK):
                turn(bank[:, block(i)], y[:, block(BLOCKS_A_BANK * h + i)], True, True)
            for i in range(BLOCKS_A_BANK):
                b = BLOCKS_A_BANK * h + i
                nc.scalar.activation(scaled[:, block(i)], bank[:, block(i)], COPY, scale=keep[:, b : b + 1])
            own_t.append(scaled)

        def product(d, start, width):
            prod = sb.tile([P, width], F32, name="prod%d_%d" % (d, start))
            if start < EARLY:
                gates = gates_early[d][:]
            else:
                gates = gates_late[d][:, start - EARLY : start - EARLY + width]
            entries = lists[d][:, start // LIST_ROWS : (start + width) // LIST_ROWS]
            nc.vector.tensor_tensor(prod[:], y[:].indirect(entries), gates, MULT)
            return prod

        def add_turned(q, prod, skip, opens, closes):
            blocks = PIECES[q][1]
            for i in range(blocks):
                turn(
                    sum_banks[q][:, block(i)],
                    prod[:, block(skip + i)],
                    opens and i == 0,
                    closes and i == blocks - 1,
                )

        def own_back(q):
            b0, blocks = PIECES[q]
            for i in range(blocks):
                h, j = divmod(b0 + i, BLOCKS_A_BANK)
                turn(out_banks[q][:, block(i)], own_t[h][:, block(j)], i == 0, False)

        def sums_out(q):
            sums = sb.tile([P, PIECES[q][1] * P], F32, name="sums%d" % q)
            nc.scalar.copy(sums[:], sum_banks[q][:, 0 : PIECES[q][1] * P])
            return sums

        def sums_back(q, sums):
            blocks = PIECES[q][1]
            for i in range(blocks):
                turn(out_banks[q][:, block(i)], sums[:, block(i)], False, i == blocks - 1)

        late_pieces = range(1, len(PIECES))

        for d in range(D):
            add_turned(0, product(d, 0, EARLY), 0, d == 0, d == D - 1)
            if d in (1, 2):
                own_back(2 * d - 2)
                own_back(2 * d - 1)

        for d in range(2):
            prod = product(d, EARLY, T - EARLY)
            for q in late_pieces:
                add_turned(q, prod, PIECES[q][0] - PIECES[0][1], d == 0, False)
            if d == 0:
                sums_back(0, sums_out(0))
                result = sb.tile([P, EARLY], F32, name="result0")
                nc.scalar.copy(result[:], out_banks[0][:, 0:EARLY])
                nc.scalar.dma_start(out=out[:, 0:EARLY], in_=result[:])

        sums = {}
        for q in late_pieces:
            b0, blocks = PIECES[q]
            add_turned(q, product(2, b0 * P, blocks * P), 0, False, True)
            sums[q] = sums_out(q)
        for q in late_pieces:
            sums_back(q, sums[q])

        prod = product(D - 1, EARLY, T - EARLY)
        for q in late_pieces:
            start, width = PIECES[q][0] * P, PIECES[q][1] * P
            result = sb.tile([P, width], F32, name="result%d" % q)
            nc.vector.tensor_tensor(
                result[:], out_banks[q][:, 0:width], prod[:, start - EARLY : start - EARLY + width], ADD
            )
            nc.sync.dma_start(out=out[:, start : start + width], in_=result[:])
